import numpy as np
import ml_dtypes


def mxq(x, axis, fmt="e4m3"):
    dtype, down = {"e4m3": (ml_dtypes.float8_e4m3fn, 7), "e5m2": (ml_dtypes.float8_e5m2, 14)}[fmt]
    v = np.moveaxis(np.asarray(x, np.float32).astype(ml_dtypes.bfloat16).astype(np.float64), axis, -1)
    blocks = v.reshape(v.shape[:-1] + (-1, 32))
    amax = np.abs(blocks).max(-1, keepdims=True)
    byte = np.maximum(np.where(amax > 0, np.frexp(amax)[1] - 1 + 127, 0) - down, 1)
    scale = np.exp2(byte - 127.0)
    codes = (blocks / scale).astype(np.float32).astype(dtype).astype(np.float64)
    return np.moveaxis((codes * scale).reshape(v.shape), -1, axis)


WIDE = False


def mx_kscale(k):
    if not WIDE:
        return np.ones(k)
    levels = np.array([10, -10, 5, -5, 0])
    if k % 512:
        return np.exp2(np.random.permutation(np.resize(levels, k // 32))).repeat(32)
    a = np.empty((k // 512, 16))
    for p in range(k // 512):
        a[p, :8] = np.random.permutation(np.resize(levels, 8))
        for g in range(8):
            far = levels[np.abs(levels - a[p, g]) >= 10]
            a[p, g + 8] = far[np.random.randint(len(far))]
    return np.exp2(a.ravel()).repeat(32)


def f64(x):
    return np.asarray(x).astype(np.float64)


def striped(idx):
    return np.tile(idx.reshape(-1, 16).T, (8, 1)).astype(np.uint16)


def unstriped(offs):
    return offs[:16].T.reshape(-1).astype(np.int64)


K, T, E, C, N = 512, 4096, 4, 256, 256


def by_expert(wq, xq):
    return np.concatenate([wq[e].T @ xq[:, e * C:(e + 1) * C] for e in range(E)], axis=1)


def setup_inputs():
    n = np.random.standard_normal
    s = mx_kscale(K)[:, None]
    return {
        "xT": (n((K, T)) * s).astype(np.float32),
        "w": (n((E, K, N)) / np.sqrt(K) / s[None]).astype(np.float32),
        "gate": np.tile(np.random.uniform(0.2, 1.0, E * C), (N, 1)).astype(np.float32),
        "offs": striped(np.random.permutation(T)[:E * C]),
    }


def reference(xT, w, gate, offs):
    idx = unstriped(offs)
    xq = mxq(f64(xT)[:, idx], 0, "e4m3")
    y = by_expert(mxq(f64(w), 1, "e4m3"), xq)
    out = np.zeros((N, T))
    out[:, idx] = f64(gate) * y
    return out

@@ -1,0 +1,155 @@
+from contextlib import ExitStack
+
+import concourse.mybir as mybir
+
+K, T, E, C, N = 512, 4096, 4, 256, 256
+FLOPS = 2 * K * N * E * C
+
+F32 = mybir.dt.float32
+BF16 = mybir.dt.bfloat16
+U32 = mybir.dt.uint32
+U16 = mybir.dt.uint16
+U8 = mybir.dt.uint8
+FP8X4 = mybir.dt.float8_e4m3fn_x4
+MULT = mybir.AluOpType.mult
+
+P = 128
+PACK = 4
+SLOTS = E * C
+HALF = SLOTS // 2
+BLOCKS = N // P
+
+
+def tile_routed_moe_kernel(tc, xT, w, gate, offs, out):
+    nc = tc.nc
+    with ExitStack() as ctx:
+        keep = ctx.enter_context(tc.tile_pool(name="keep", bufs=1))
+        psum = ctx.enter_context(tc.psum_pool(name="psum", bufs=1))
+
+        offsets = keep.tile([P, SLOTS // 16], U16, name="offsets")
+
+        x_view = xT.rearrange("(p t) n -> p t n", t=PACK)
+        planes = []
+        for t in range(PACK):
+            plane = keep.tile([P, T], F32, name="plane%d" % t)
+            nc.sync.dma_start(plane[:], x_view[:, t, :])
+            planes.append(plane)
+            if t == 0:
+                nc.sync.dma_start(offsets[:], offs)
+
+        w_view = w.rearrange("e (p j) n -> e p j n", j=PACK)
+        w_raw = [[keep.tile([P, PACK, P], F32, name="w_raw%d%d" % (b, e)) for e in range(E)] for b in range(BLOCKS)]
+        gates = [[keep.tile([P, HALF], F32, name="gate%d%d" % (b, h)) for h in range(2)] for b in range(BLOCKS)]
+
+        def load_w(b, e):
+            nc.sync.dma_start(w_raw[b][e][:], w_view[e][:, :, b * P : (b + 1) * P])
+
+        def load_gate(b, h):
+            nc.sync.dma_start(gates[b][h][:], gate[b * P : (b + 1) * P, h * HALF : (h + 1) * HALF])
+
+        for e in range(E):
+            load_w(0, e)
+        load_gate(0, 0)
+        for e in range(E):
+            load_w(1, e)
+        load_gate(0, 1)
+        load_gate(1, 0)
+        load_gate(1, 1)
+
+        windows = []
+        for b in range(BLOCKS):
+            window = keep.tile([P, T], F32, name="window%d" % b)
+            nc.vector.memset(window[:], 0.0)
+            windows.append(window)
+
+        x_grouped = keep.tile([P, SLOTS, PACK], BF16, name="x_grouped", align_bytes=64)
+        x_codes = keep.tile([P, SLOTS], U32, name="x_codes", align_bytes=64)
+        x_scales = keep.tile([P, SLOTS], U8, name="x_scales", align_bytes=64)
+        w_grouped = keep.tile([P, BLOCKS, E, P, PACK], BF16, name="w_grouped", align_bytes=64)
+        w_codes = keep.tile([P, BLOCKS * E * P], U32, name="w_codes", align_bytes=64)
+        w_scales = keep.tile([P, BLOCKS * E * P], U8, name="w_scales", align_bytes=64)
+
+        def list_half(h):
+            return offsets[:, h * (HALF // 16) : (h + 1) * (HALF // 16)]
+
+        def gather(t, h):
+            nc.vector.tensor_copy(
+                out=x_grouped[:, h * HALF : (h + 1) * HALF, t],
+                in_=planes[t][:].indirect(list_half(h)),
+            )
+
+        def quantize_x(h):
+            cols = slice(h * HALF, (h + 1) * HALF)
+            nc.vector.quantize_mx(
+                out=x_codes[:, cols].bitcast(FP8X4),
+                scales=x_scales[:, cols],
+                in_=x_grouped[:, cols, :].rearrange("p s t -> p (s t)"),
+            )
+
+        def interleave_w(b, e):
+            nc.scalar.copy(
+                out=w_grouped[:, b, e].rearrange("p (c i) j -> p c j i", i=4),
+                in_=w_raw[b][e][:].rearrange("p j (c i) -> p c j i", i=4),
+            )
+
+        def quantize_w(b, e0, e1):
+            cols = slice((b * E + e0) * P, (b * E + e1) * P)
+            nc.vector.quantize_mx(
+                out=w_codes[:, cols].bitcast(FP8X4),
+                scales=w_scales[:, cols],
+                in_=w_grouped[:, b, e0:e1].rearrange("p e n j -> p (e n j)"),
+            )
+
+        def multiply(b, h):
+            acc = psum.tile([P, HALF], F32, name="acc%d%d" % (b, h))
+            for i in range(2):
+                e = 2 * h + i
+                feat = slice((b * E + e) * P, (b * E + e + 1) * P)
+                slots = slice(e * C, (e + 1) * C)
+                nc.tensor.matmul_mx(
+                    out=acc[:, i * C : (i + 1) * C],
+                    lhsT=w_codes[:, feat].bitcast(FP8X4),
+                    lhsT_scale=w_scales[:, feat],
+                    rhs=x_codes[:, slots].bitcast(FP8X4),
+                    rhs_scale=x_scales[:, slots],
+                    start=True,
+                    stop=True,
+                )
+            y = keep.tile([P, HALF], F32, name="y%d%d" % (b, h))
+            nc.scalar.copy(out=y[:], in_=acc[:])
+            return y
+
+        def scatter(b, h, y):
+            nc.vector.tensor_tensor(
+                out=windows[b][:].indirect(list_half(h)), in0=y[:], in1=gates[b][h][:], op=MULT
+            )
+
+        for t in range(PACK - 1):
+            for h in range(2):
+                gather(t, h)
+        gather(PACK - 1, 0)
+        quantize_x(0)
+        interleave_w(0, 0)
+        interleave_w(0, 1)
+        quantize_w(0, 0, 2)
+        y00 = multiply(0, 0)
+        gather(PACK - 1, 1)
+        quantize_x(1)
+        interleave_w(0, 2)
+        interleave_w(0, 3)
+        quantize_w(0, 2, 4)
+        y01 = multiply(0, 1)
+        scatter(0, 0, y00)
+        interleave_w(1, 0)
+        interleave_w(1, 1)
+        quantize_w(1, 0, 2)
+        y10 = multiply(1, 0)
+        scatter(0, 1, y01)
+        nc.sync.dma_start(out[0:P, :], windows[0][:])
+        interleave_w(1, 2)
+        interleave_w(1, 3)
+        quantize_w(1, 2, 4)
+        y11 = multiply(1, 1)
+        scatter(1, 0, y10)
+        scatter(1, 1, y11)
+        nc.sync.dma_start(out[P : 2 * P, :], windows[1][:])

@@ -63,7 +63,8 @@ def tile_routed_moe_kernel(tc, xT, w, gate, offs, out):
             windows.append(window)
 
         x_grouped = keep.tile([P, SLOTS, PACK], BF16, name="x_grouped", align_bytes=64)
-        x_codes = keep.tile([P, SLOTS], U32, name="x_codes", align_bytes=64)
+        x_codes = [keep.tile([P, HALF], U32, name="x_codes0", align_bytes=64)]
+        w_first = keep.tile([P, 2, P, PACK], BF16, name="w_first", tag="turn", align_bytes=64)
         x_scales = keep.tile([P, SLOTS], U8, name="x_scales", align_bytes=64)
         w_grouped = keep.tile([P, BLOCKS, E, P, PACK], BF16, name="w_grouped", align_bytes=64)
         w_codes = keep.tile([P, BLOCKS * E * P], U32, name="w_codes", align_bytes=64)
@@ -81,14 +82,20 @@ def tile_routed_moe_kernel(tc, xT, w, gate, offs, out):
         def quantize_x(h):
             cols = slice(h * HALF, (h + 1) * HALF)
             nc.vector.quantize_mx(
-                out=x_codes[:, cols].bitcast(FP8X4),
+                out=x_codes[h][:].bitcast(FP8X4),
                 scales=x_scales[:, cols],
                 in_=x_grouped[:, cols, :].rearrange("p s t -> p (s t)"),
             )
 
+        def staged(b, e0, e1):
+            return w_first[:, e0:e1] if (b == 0 and e1 <= 2) else w_grouped[:, b, e0:e1]
+
+        def staged_one(b, e):
+            return w_first[:, e] if (b == 0 and e < 2) else w_grouped[:, b, e]
+
         def interleave_w(b, e):
             nc.scalar.copy(
-                out=w_grouped[:, b, e].rearrange("p (c i) j -> p c j i", i=4),
+                out=staged_one(b, e).rearrange("p (c i) j -> p c j i", i=4),
                 in_=w_raw[b][e][:].rearrange("p j (c i) -> p c j i", i=4),
             )
 
@@ -97,7 +104,7 @@ def tile_routed_moe_kernel(tc, xT, w, gate, offs, out):
             nc.vector.quantize_mx(
                 out=w_codes[:, cols].bitcast(FP8X4),
                 scales=w_scales[:, cols],
-                in_=w_grouped[:, b, e0:e1].rearrange("p e n j -> p (e n j)"),
+                in_=staged(b, e0, e1).rearrange("p e n j -> p (e n j)"),
             )
 
         def multiply(b, h):
@@ -106,11 +113,12 @@ def tile_routed_moe_kernel(tc, xT, w, gate, offs, out):
                 e = 2 * h + i
                 feat = slice((b * E + e) * P, (b * E + e + 1) * P)
                 slots = slice(e * C, (e + 1) * C)
+                part = slice(i * C, (i + 1) * C)
                 nc.tensor.matmul_mx(
                     out=acc[:, i * C : (i + 1) * C],
                     lhsT=w_codes[:, feat].bitcast(FP8X4),
                     lhsT_scale=w_scales[:, feat],
-                    rhs=x_codes[:, slots].bitcast(FP8X4),
+                    rhs=x_codes[h][:, part].bitcast(FP8X4),
                     rhs_scale=x_scales[:, slots],
                     start=True,
                     stop=True,
@@ -133,6 +141,7 @@ def tile_routed_moe_kernel(tc, xT, w, gate, offs, out):
         interleave_w(0, 1)
         quantize_w(0, 0, 2)
         y00 = multiply(0, 0)
+        x_codes.append(keep.tile([P, HALF], U32, name="x_codes1", tag="turn", align_bytes=64))
         gather(PACK - 1, 1)
         quantize_x(1)
         interleave_w(0, 2)

@@ -107,6 +107,26 @@ def tile_routed_moe_kernel(tc, xT, w, gate, offs, out):
                 in_=staged(b, e0, e1).rearrange("p e n j -> p (e n j)"),
             )
 
+        def multiply_by_expert(b, h):
+            y = keep.tile([P, HALF], F32, name="y%d%d" % (b, h))
+            for i in range(2):
+                e = 2 * h + i
+                feat = slice((b * E + e) * P, (b * E + e + 1) * P)
+                slots = slice(e * C, (e + 1) * C)
+                part = slice(i * C, (i + 1) * C)
+                acc = psum.tile([P, HALF], F32, name="acc%d%d%d" % (b, h, i))
+                nc.tensor.matmul_mx(
+                    out=acc[:, 0:C],
+                    lhsT=w_codes[:, feat].bitcast(FP8X4),
+                    lhsT_scale=w_scales[:, feat],
+                    rhs=x_codes[h][:, part].bitcast(FP8X4),
+                    rhs_scale=x_scales[:, slots],
+                    start=True,
+                    stop=True,
+                )
+                nc.scalar.copy(out=y[:, part], in_=acc[:, 0:C])
+            return y
+
         def multiply(b, h):
             acc = psum.tile([P, HALF], F32, name="acc%d%d" % (b, h))
             for i in range(2):
@@ -140,7 +160,7 @@ def tile_routed_moe_kernel(tc, xT, w, gate, offs, out):
         interleave_w(0, 0)
         interleave_w(0, 1)
         quantize_w(0, 0, 2)
-        y00 = multiply(0, 0)
+        y00 = multiply_by_expert(0, 0)
         x_codes.append(keep.tile([P, HALF], U32, name="x_codes1", tag="turn", align_bytes=64))
         gather(PACK - 1, 1)
         quantize_x(1)

@@ -63,7 +63,7 @@ def tile_routed_moe_kernel(tc, xT, w, gate, offs, out):
             windows.append(window)
 
         x_grouped = keep.tile([P, SLOTS, PACK], BF16, name="x_grouped", align_bytes=64)
-        x_codes = [keep.tile([P, HALF], U32, name="x_codes0", align_bytes=64)]
+        x_codes = []
         w_first = keep.tile([P, 2, P, PACK], BF16, name="w_first", tag="turn", align_bytes=64)
         x_scales = keep.tile([P, SLOTS], U8, name="x_scales", align_bytes=64)
         w_grouped = keep.tile([P, BLOCKS, E, P, PACK], BF16, name="w_grouped", align_bytes=64)
@@ -79,10 +79,10 @@ def tile_routed_moe_kernel(tc, xT, w, gate, offs, out):
                 in_=planes[t][:].indirect(list_half(h)),
             )
 
-        def quantize_x(h):
-            cols = slice(h * HALF, (h + 1) * HALF)
+        def quantize_x(s0, s1):
+            cols = slice(s0, s1)
             nc.vector.quantize_mx(
-                out=x_codes[h][:].bitcast(FP8X4),
+                out=x_codes[0][:, cols].bitcast(FP8X4),
                 scales=x_scales[:, cols],
                 in_=x_grouped[:, cols, :].rearrange("p s t -> p (s t)"),
             )
@@ -119,7 +119,7 @@ def tile_routed_moe_kernel(tc, xT, w, gate, offs, out):
                     out=acc[:, 0:C],
                     lhsT=w_codes[:, feat].bitcast(FP8X4),
                     lhsT_scale=w_scales[:, feat],
-                    rhs=x_codes[h][:, part].bitcast(FP8X4),
+                    rhs=x_codes[0][:, slots].bitcast(FP8X4),
                     rhs_scale=x_scales[:, slots],
                     start=True,
                     stop=True,
@@ -138,7 +138,7 @@ def tile_routed_moe_kernel(tc, xT, w, gate, offs, out):
                     out=acc[:, i * C : (i + 1) * C],
                     lhsT=w_codes[:, feat].bitcast(FP8X4),
                     lhsT_scale=w_scales[:, feat],
-                    rhs=x_codes[h][:, part].bitcast(FP8X4),
+                    rhs=x_codes[0][:, slots].bitcast(FP8X4),
                     rhs_scale=x_scales[:, slots],
                     start=True,
                     stop=True,
@@ -155,15 +155,16 @@ def tile_routed_moe_kernel(tc, xT, w, gate, offs, out):
         for t in range(PACK - 1):
             for h in range(2):
                 gather(t, h)
-        gather(PACK - 1, 0)
-        quantize_x(0)
         interleave_w(0, 0)
         interleave_w(0, 1)
         quantize_w(0, 0, 2)
+        x_codes.append(keep.tile([P, SLOTS], U32, name="x_codes", tag="turn", align_bytes=64))
+        gather(PACK - 1, 0)
+        quantize_x(0, C)
+        quantize_x(C, 2 * C)
         y00 = multiply_by_expert(0, 0)
-        x_codes.append(keep.tile([P, HALF], U32, name="x_codes1", tag="turn", align_bytes=64))
         gather(PACK - 1, 1)
-        quantize_x(1)
+        quantize_x(HALF, SLOTS)
         interleave_w(0, 2)
         interleave_w(0, 3)
         quantize_w(0, 2, 4)

@@ -38,23 +38,25 @@ def tile_routed_moe_kernel(tc, xT, w, gate, offs, out):
                 nc.sync.dma_start(offsets[:], offs)
 
         w_view = w.rearrange("e (p j) n -> e p j n", j=PACK)
-        w_raw = [[keep.tile([P, PACK, P], F32, name="w_raw%d%d" % (b, e)) for e in range(E)] for b in range(BLOCKS)]
-        gates = [[keep.tile([P, HALF], F32, name="gate%d%d" % (b, h)) for h in range(2)] for b in range(BLOCKS)]
+        w_raw = [[keep.tile([P, PACK, P], F32, name="w_raw%d%d" % (b, e)) for e in range(E)] for b in range(BLOCKS - 1)]
+        w_raw.append([keep.tile([P, PACK, P], F32, name="w_raw1%d" % e) for e in range(E - 1)])
+        w_raw[1].append(keep.tile([P, PACK, P], F32, name="w_raw13", tag="late"))
+        gates = [keep.tile([P, HALF], F32, name="gate00"), keep.tile([P, HALF], F32, name="gate01")]
+        gate1 = keep.tile([P, SLOTS], F32, name="gate1")
 
         def load_w(b, e):
             nc.sync.dma_start(w_raw[b][e][:], w_view[e][:, :, b * P : (b + 1) * P])
 
-        def load_gate(b, h):
-            nc.sync.dma_start(gates[b][h][:], gate[b * P : (b + 1) * P, h * HALF : (h + 1) * HALF])
+        def load_gate(h):
+            nc.sync.dma_start(gates[h][:], gate[0:P, h * HALF : (h + 1) * HALF])
 
         for e in range(E):
             load_w(0, e)
-        load_gate(0, 0)
+        load_gate(0)
         for e in range(E):
             load_w(1, e)
-        load_gate(0, 1)
-        load_gate(1, 0)
-        load_gate(1, 1)
+        load_gate(1)
+        nc.sync.dma_start(gate1[:], gate[P : 2 * P, :])
 
         windows = []
         for b in range(BLOCKS):
@@ -127,7 +129,7 @@ def tile_routed_moe_kernel(tc, xT, w, gate, offs, out):
                 nc.scalar.copy(out=y[:, part], in_=acc[:, 0:C])
             return y
 
-        def multiply(b, h):
+        def multiply(b, h, y):
             acc = psum.tile([P, HALF], F32, name="acc%d%d" % (b, h))
             for i in range(2):
                 e = 2 * h + i
@@ -143,13 +145,11 @@ def tile_routed_moe_kernel(tc, xT, w, gate, offs, out):
                     start=True,
                     stop=True,
                 )
-            y = keep.tile([P, HALF], F32, name="y%d%d" % (b, h))
-            nc.scalar.copy(out=y[:], in_=acc[:])
-            return y
+            nc.scalar.copy(out=y, in_=acc[:])
 
-        def scatter(b, h, y):
+        def scatter(h, y):
             nc.vector.tensor_tensor(
-                out=windows[b][:].indirect(list_half(h)), in0=y[:], in1=gates[b][h][:], op=MULT
+                out=windows[0][:].indirect(list_half(h)), in0=y[:], in1=gates[h][:], op=MULT
             )
 
         for t in range(PACK - 1):
@@ -168,18 +168,16 @@ def tile_routed_moe_kernel(tc, xT, w, gate, offs, out):
         interleave_w(0, 2)
         interleave_w(0, 3)
         quantize_w(0, 2, 4)
-        y01 = multiply(0, 1)
-        scatter(0, 0, y00)
-        interleave_w(1, 0)
-        interleave_w(1, 1)
-        quantize_w(1, 0, 2)
-        y10 = multiply(1, 0)
-        scatter(0, 1, y01)
+        scatter(0, y00)
+        for e in range(E):
+            interleave_w(1, e)
+        y01 = keep.tile([P, HALF], F32, name="y01", tag="late")
+        multiply(0, 1, y01[:])
+        quantize_w(1, 0, 4)
+        y1 = keep.tile([P, SLOTS], F32, name="y1")
+        for h in range(2):
+            multiply(1, h, y1[:, h * HALF : (h + 1) * HALF])
+        scatter(1, y01)
         nc.sync.dma_start(out[0:P, :], windows[0][:])
-        interleave_w(1, 2)
-        interleave_w(1, 3)
-        quantize_w(1, 2, 4)
-        y11 = multiply(1, 1)
-        scatter(1, 0, y10)
-        scatter(1, 1, y11)
+        nc.vector.tensor_tensor(out=windows[1][:].indirect(offsets[:]), in0=y1[:], in1=gate1[:], op=MULT)
         nc.sync.dma_start(out[P : 2 * P, :], windows[1][:])

@@ -38,7 +38,7 @@ def tile_routed_moe_kernel(tc, xT, w, gate, offs, out):
                 nc.sync.dma_start(offsets[:], offs)
 
         w_view = w.rearrange("e (p j) n -> e p j n", j=PACK)
-        w_raw = [[keep.tile([P, PACK, P], F32, name="w_raw%d%d" % (b, e)) for e in range(E)] for b in range(BLOCKS - 1)]
+        w_raw = [[keep.tile([P, PACK, P], F32, name="w_raw0%d" % e, tag="turn" if e == 1 else "w_raw0%d" % e, align_bytes=64) for e in range(E)]]
         w_raw.append([keep.tile([P, PACK, P], F32, name="w_raw1%d" % e) for e in range(E - 1)])
         w_raw[1].append(keep.tile([P, PACK, P], F32, name="w_raw13", tag="late"))
         gates = [keep.tile([P, HALF], F32, name="gate00"), keep.tile([P, HALF], F32, name="gate01")]
@@ -66,7 +66,6 @@ def tile_routed_moe_kernel(tc, xT, w, gate, offs, out):
 
         x_grouped = keep.tile([P, SLOTS, PACK], BF16, name="x_grouped", align_bytes=64)
         x_codes = []
-        w_first = keep.tile([P, 2, P, PACK], BF16, name="w_first", tag="turn", align_bytes=64)
         x_scales = keep.tile([P, SLOTS], U8, name="x_scales", align_bytes=64)
         w_grouped = keep.tile([P, BLOCKS, E, P, PACK], BF16, name="w_grouped", align_bytes=64)
         w_codes = keep.tile([P, BLOCKS * E * P], U32, name="w_codes", align_bytes=64)
@@ -89,15 +88,9 @@ def tile_routed_moe_kernel(tc, xT, w, gate, offs, out):
                 in_=x_grouped[:, cols, :].rearrange("p s t -> p (s t)"),
             )
 
-        def staged(b, e0, e1):
-            return w_first[:, e0:e1] if (b == 0 and e1 <= 2) else w_grouped[:, b, e0:e1]
-
-        def staged_one(b, e):
-            return w_first[:, e] if (b == 0 and e < 2) else w_grouped[:, b, e]
-
         def interleave_w(b, e):
             nc.scalar.copy(
-                out=staged_one(b, e).rearrange("p (c i) j -> p c j i", i=4),
+                out=w_grouped[:, b, e].rearrange("p (c i) j -> p c j i", i=4),
                 in_=w_raw[b][e][:].rearrange("p j (c i) -> p c j i", i=4),
             )
 
@@ -106,7 +99,7 @@ def tile_routed_moe_kernel(tc, xT, w, gate, offs, out):
             nc.vector.quantize_mx(
                 out=w_codes[:, cols].bitcast(FP8X4),
                 scales=w_scales[:, cols],
-                in_=staged(b, e0, e1).rearrange("p e n j -> p (e n j)"),
+                in_=w_grouped[:, b, e0:e1].rearrange("p e n j -> p (e n j)"),
             )
 
         def multiply_by_expert(b, h):

@@ -19,6 +19,11 @@ SLOTS = E * C
 HALF = SLOTS // 2
 BLOCKS = N // P
 
+X_AT = 2 * P
+W23_AT = X_AT + SLOTS
+MIX = W23_AT + 2 * P
+FIRST = X_AT + C
+
 
 def tile_routed_moe_kernel(tc, xT, w, gate, offs, out):
     nc = tc.nc
@@ -38,14 +43,20 @@ def tile_routed_moe_kernel(tc, xT, w, gate, offs, out):
                 nc.sync.dma_start(offsets[:], offs)
 
         w_view = w.rearrange("e (p j) n -> e p j n", j=PACK)
-        w_raw = [[keep.tile([P, PACK, P], F32, name="w_raw0%d" % e, tag="turn" if e == 1 else "w_raw0%d" % e, align_bytes=64) for e in range(E)]]
-        w_raw.append([keep.tile([P, PACK, P], F32, name="w_raw1%d" % e) for e in range(E - 1)])
-        w_raw[1].append(keep.tile([P, PACK, P], F32, name="w_raw13", tag="late"))
-        gates = [keep.tile([P, HALF], F32, name="gate00"), keep.tile([P, HALF], F32, name="gate01")]
+        shared = {(0, 2): "turn", (1, 3): "late"}
+        w_raw_pair = keep.tile([P, 2, PACK, P], F32, name="w_raw_pair")
+        w_raw = {(1, 0): w_raw_pair[:, 0], (1, 1): w_raw_pair[:, 1]}
+        for b in range(BLOCKS):
+            for e in range(E):
+                if (b, e) not in w_raw:
+                    name = "w_raw%d%d" % (b, e)
+                    raw = keep.tile([P, PACK, P], F32, name=name, tag=shared.get((b, e), name), align_bytes=64)
+                    w_raw[b, e] = raw[:]
+        gates = [keep.tile([P, HALF], F32, name="gate0%d" % h) for h in range(2)]
         gate1 = keep.tile([P, SLOTS], F32, name="gate1")
 
         def load_w(b, e):
-            nc.sync.dma_start(w_raw[b][e][:], w_view[e][:, :, b * P : (b + 1) * P])
+            nc.sync.dma_start(w_raw[b, e], w_view[e][:, :, b * P : (b + 1) * P])
 
         def load_gate(h):
             nc.sync.dma_start(gates[h][:], gate[0:P, h * HALF : (h + 1) * HALF])
@@ -64,80 +75,70 @@ def tile_routed_moe_kernel(tc, xT, w, gate, offs, out):
             nc.vector.memset(window[:], 0.0)
             windows.append(window)
 
-        x_grouped = keep.tile([P, SLOTS, PACK], BF16, name="x_grouped", align_bytes=64)
-        x_codes = []
-        x_scales = keep.tile([P, SLOTS], U8, name="x_scales", align_bytes=64)
-        w_grouped = keep.tile([P, BLOCKS, E, P, PACK], BF16, name="w_grouped", align_bytes=64)
-        w_codes = keep.tile([P, BLOCKS * E * P], U32, name="w_codes", align_bytes=64)
-        w_scales = keep.tile([P, BLOCKS * E * P], U8, name="w_scales", align_bytes=64)
+        mix = keep.tile([P, MIX, PACK], BF16, name="mix", tag="grouped", align_bytes=64)
+        mix_scales = keep.tile([P, MIX], U8, name="mix_scales", align_bytes=64)
+        w1_codes = keep.tile([P, E * P], U32, name="w1_codes", align_bytes=64)
+        w1_scales = keep.tile([P, E * P], U8, name="w1_scales", align_bytes=64)
 
         def list_half(h):
             return offsets[:, h * (HALF // 16) : (h + 1) * (HALF // 16)]
 
         def gather(t, h):
-            nc.vector.tensor_copy(
-                out=x_grouped[:, h * HALF : (h + 1) * HALF, t],
-                in_=planes[t][:].indirect(list_half(h)),
-            )
+            at = X_AT + h * HALF
+            nc.vector.tensor_copy(out=mix[:, at : at + HALF, t], in_=planes[t][:].indirect(list_half(h)))
 
-        def quantize_x(s0, s1):
-            cols = slice(s0, s1)
-            nc.vector.quantize_mx(
-                out=x_codes[0][:, cols].bitcast(FP8X4),
-                scales=x_scales[:, cols],
-                in_=x_grouped[:, cols, :].rearrange("p s t -> p (s t)"),
-            )
+        def w_at(b, e):
+            if b == 1:
+                return e * P
+            return e * P if e < 2 else W23_AT + (e - 2) * P
 
         def interleave_w(b, e):
+            at = w_at(b, e)
+            grouped = mix if b == 0 else w1
             nc.scalar.copy(
-                out=w_grouped[:, b, e].rearrange("p (c i) j -> p c j i", i=4),
-                in_=w_raw[b][e][:].rearrange("p j (c i) -> p c j i", i=4),
+                out=grouped[:, at : at + P, :].rearrange("p (c i) j -> p c j i", i=4),
+                in_=w_raw[b, e].rearrange("p j (c i) -> p c j i", i=4),
             )
 
-        def quantize_w(b, e0, e1):
-            cols = slice((b * E + e0) * P, (b * E + e1) * P)
+        def interleave_pair():
+            nc.scalar.copy(
+                out=w1[:, 0 : 2 * P, :].rearrange("p (e c i) j -> p e c j i", e=2, i=4),
+                in_=w_raw_pair[:].rearrange("p e j (c i) -> p e c j i", i=4),
+            )
+
+        def codes_of(b, at, end):
+            if b == 1:
+                return w1_codes[:, at:end].bitcast(FP8X4)
+            if end <= FIRST:
+                return first_codes[:, at:end].bitcast(FP8X4)
+            return rest_codes[:, at - FIRST : end - FIRST].bitcast(FP8X4)
+
+        def quantize(b, at, end):
+            grouped, scales = (mix, mix_scales) if b == 0 else (w1, w1_scales)
             nc.vector.quantize_mx(
-                out=w_codes[:, cols].bitcast(FP8X4),
-                scales=w_scales[:, cols],
-                in_=w_grouped[:, b, e0:e1].rearrange("p e n j -> p (e n j)"),
+                out=codes_of(b, at, end),
+                scales=scales[:, at:end],
+                in_=grouped[:, at:end, :].rearrange("p s t -> p (s t)"),
             )
 
-        def multiply_by_expert(b, h):
-            y = keep.tile([P, HALF], F32, name="y%d%d" % (b, h))
-            for i in range(2):
-                e = 2 * h + i
-                feat = slice((b * E + e) * P, (b * E + e + 1) * P)
-                slots = slice(e * C, (e + 1) * C)
-                part = slice(i * C, (i + 1) * C)
-                acc = psum.tile([P, HALF], F32, name="acc%d%d%d" % (b, h, i))
-                nc.tensor.matmul_mx(
-                    out=acc[:, 0:C],
-                    lhsT=w_codes[:, feat].bitcast(FP8X4),
-                    lhsT_scale=w_scales[:, feat],
-                    rhs=x_codes[0][:, slots].bitcast(FP8X4),
-                    rhs_scale=x_scales[:, slots],
-                    start=True,
-                    stop=True,
-                )
-                nc.scalar.copy(out=y[:, part], in_=acc[:, 0:C])
-            return y
+        def multiply(b, e, acc):
+            w_scales = mix_scales if b == 0 else w1_scales
+            feat = slice(w_at(b, e), w_at(b, e) + P)
+            slots = slice(X_AT + e * C, X_AT + (e + 1) * C)
+            nc.tensor.matmul_mx(
+                out=acc,
+                lhsT=codes_of(b, feat.start, feat.stop),
+                lhsT_scale=w_scales[:, feat],
+                rhs=codes_of(0, slots.start, slots.stop),
+                rhs_scale=mix_scales[:, slots],
+                start=True,
+                stop=True,
+            )
 
-        def multiply(b, h, y):
+        def multiply_half(b, h, y):
             acc = psum.tile([P, HALF], F32, name="acc%d%d" % (b, h))
             for i in range(2):
-                e = 2 * h + i
-                feat = slice((b * E + e) * P, (b * E + e + 1) * P)
-                slots = slice(e * C, (e + 1) * C)
-                part = slice(i * C, (i + 1) * C)
-                nc.tensor.matmul_mx(
-                    out=acc[:, i * C : (i + 1) * C],
-                    lhsT=w_codes[:, feat].bitcast(FP8X4),
-                    lhsT_scale=w_scales[:, feat],
-                    rhs=x_codes[0][:, slots].bitcast(FP8X4),
-                    rhs_scale=x_scales[:, slots],
-                    start=True,
-                    stop=True,
-                )
+                multiply(b, 2 * h + i, acc[:, i * C : (i + 1) * C])
             nc.scalar.copy(out=y, in_=acc[:])
 
         def scatter(h, y):
@@ -145,31 +146,35 @@ def tile_routed_moe_kernel(tc, xT, w, gate, offs, out):
                 out=windows[0][:].indirect(list_half(h)), in0=y[:], in1=gates[h][:], op=MULT
             )
 
-        for t in range(PACK - 1):
+        for t in range(PACK):
             for h in range(2):
                 gather(t, h)
         interleave_w(0, 0)
         interleave_w(0, 1)
-        quantize_w(0, 0, 2)
-        x_codes.append(keep.tile([P, SLOTS], U32, name="x_codes", tag="turn", align_bytes=64))
-        gather(PACK - 1, 0)
-        quantize_x(0, C)
-        quantize_x(C, 2 * C)
-        y00 = multiply_by_expert(0, 0)
-        gather(PACK - 1, 1)
-        quantize_x(HALF, SLOTS)
+        first_codes = keep.tile([P, FIRST], U32, name="first_codes", align_bytes=64)
+        quantize(0, 0, FIRST)
         interleave_w(0, 2)
+        rest_codes = keep.tile([P, MIX - FIRST], U32, name="rest_codes", tag="turn", align_bytes=64)
+        quantize(0, FIRST, FIRST + C)
+        y00 = keep.tile([P, HALF], F32, name="y00")
+        for e in range(2):
+            acc = psum.tile([P, HALF], F32, name="acc00%d" % e)
+            multiply(0, e, acc[:, 0:C])
+            nc.scalar.copy(out=y00[:, e * C : (e + 1) * C], in_=acc[:, 0:C])
+        quantize(0, FIRST + C, W23_AT)
         interleave_w(0, 3)
-        quantize_w(0, 2, 4)
+        quantize(0, W23_AT, MIX)
         scatter(0, y00)
-        for e in range(E):
+        w1 = keep.tile([P, E * P, PACK], BF16, name="w1", tag="grouped", align_bytes=64)
+        interleave_pair()
+        for e in range(2, E):
             interleave_w(1, e)
-        y01 = keep.tile([P, HALF], F32, name="y01", tag="late")
-        multiply(0, 1, y01[:])
-        quantize_w(1, 0, 4)
+        y01 = keep.tile([P, HALF], F32, name="y01", tag="late", align_bytes=64)
+        multiply_half(0, 1, y01[:])
+        quantize(1, 0, E * P)
         y1 = keep.tile([P, SLOTS], F32, name="y1")
         for h in range(2):
-            multiply(1, h, y1[:, h * HALF : (h + 1) * HALF])
+            multiply_half(1, h, y1[:, h * HALF : (h + 1) * HALF])
         scatter(1, y01)
         nc.sync.dma_start(out[0:P, :], windows[0][:])
         nc.vector.tensor_tensor(out=windows[1][:].indirect(offsets[:]), in0=y1[:], in1=gate1[:], op=MULT)

@@ -37,7 +37,9 @@ def tile_routed_moe_kernel(tc, xT, w, gate, offs, out):
         planes = []
         for t in range(PACK):
             plane = keep.tile([P, T], F32, name="plane%d" % t)
-            nc.sync.dma_start(plane[:], x_view[:, t, :])
+            for c in range(2):
+                half = slice(c * (T // 2), (c + 1) * (T // 2))
+                nc.sync.dma_start(plane[:, half], x_view[:, t, half])
             planes.append(plane)
             if t == 0:
                 nc.sync.dma_start(offsets[:], offs)

from contextlib import ExitStack

import concourse.mybir as mybir

K, T, E, C, N = 512, 4096, 4, 256, 256
FLOPS = 2 * K * N * E * C

F32 = mybir.dt.float32
BF16 = mybir.dt.bfloat16
U32 = mybir.dt.uint32
U16 = mybir.dt.uint16
U8 = mybir.dt.uint8
FP8X4 = mybir.dt.float8_e4m3fn_x4
MULT = mybir.AluOpType.mult

P = 128
PACK = 4
SLOTS = E * C
HALF = SLOTS // 2
BLOCKS = N // P

X_AT = 2 * P
W23_AT = X_AT + SLOTS
MIX = W23_AT + 2 * P
FIRST = X_AT + C


def tile_routed_moe_kernel(tc, xT, w, gate, offs, out):
    nc = tc.nc
    with ExitStack() as ctx:
        keep = ctx.enter_context(tc.tile_pool(name="keep", bufs=1))
        psum = ctx.enter_context(tc.psum_pool(name="psum", bufs=1))

        offsets = keep.tile([P, SLOTS // 16], U16, name="offsets")

        x_view = xT.rearrange("(p t) n -> p t n", t=PACK)
        planes = []
        for t in range(PACK):
            plane = keep.tile([P, T], F32, name="plane%d" % t)
            for c in range(2):
                half = slice(c * (T // 2), (c + 1) * (T // 2))
                nc.sync.dma_start(plane[:, half], x_view[:, t, half])
            planes.append(plane)
            if t == 0:
                nc.sync.dma_start(offsets[:], offs)

        w_view = w.rearrange("e (p j) n -> e p j n", j=PACK)
        shared = {(0, 2): "turn", (1, 3): "late"}
        w_raw_pair = keep.tile([P, 2, PACK, P], F32, name="w_raw_pair")
        w_raw = {(1, 0): w_raw_pair[:, 0], (1, 1): w_raw_pair[:, 1]}
        for b in range(BLOCKS):
            for e in range(E):
                if (b, e) not in w_raw:
                    name = "w_raw%d%d" % (b, e)
                    raw = keep.tile([P, PACK, P], F32, name=name, tag=shared.get((b, e), name), align_bytes=64)
                    w_raw[b, e] = raw[:]
        gates = [keep.tile([P, HALF], F32, name="gate0%d" % h) for h in range(2)]
        gate1 = keep.tile([P, SLOTS], F32, name="gate1")

        def load_w(b, e):
            nc.sync.dma_start(w_raw[b, e], w_view[e][:, :, b * P : (b + 1) * P])

        def load_gate(h):
            nc.sync.dma_start(gates[h][:], gate[0:P, h * HALF : (h + 1) * HALF])

        for e in range(E):
            load_w(0, e)
        load_gate(0)
        for e in range(E):
            load_w(1, e)
        load_gate(1)
        nc.sync.dma_start(gate1[:], gate[P : 2 * P, :])

        windows = []
        for b in range(BLOCKS):
            window = keep.tile([P, T], F32, name="window%d" % b)
            nc.vector.memset(window[:], 0.0)
            windows.append(window)

        mix = keep.tile([P, MIX, PACK], BF16, name="mix", tag="grouped", align_bytes=64)
        mix_scales = keep.tile([P, MIX], U8, name="mix_scales", align_bytes=64)
        w1_codes = keep.tile([P, E * P], U32, name="w1_codes", align_bytes=64)
        w1_scales = keep.tile([P, E * P], U8, name="w1_scales", align_bytes=64)

        def list_half(h):
            return offsets[:, h * (HALF // 16) : (h + 1) * (HALF // 16)]

        def gather(t, h):
            at = X_AT + h * HALF
            nc.vector.tensor_copy(out=mix[:, at : at + HALF, t], in_=planes[t][:].indirect(list_half(h)))

        def w_at(b, e):
            if b == 1:
                return e * P
            return e * P if e < 2 else W23_AT + (e - 2) * P

        def interleave_w(b, e):
            at = w_at(b, e)
            grouped = mix if b == 0 else w1
            nc.scalar.copy(
                out=grouped[:, at : at + P, :].rearrange("p (c i) j -> p c j i", i=4),
                in_=w_raw[b, e].rearrange("p j (c i) -> p c j i", i=4),
            )

        def interleave_pair():
            nc.scalar.copy(
                out=w1[:, 0 : 2 * P, :].rearrange("p (e c i) j -> p e c j i", e=2, i=4),
                in_=w_raw_pair[:].rearrange("p e j (c i) -> p e c j i", i=4),
            )

        def codes_of(b, at, end):
            if b == 1:
                return w1_codes[:, at:end].bitcast(FP8X4)
            if end <= FIRST:
                return first_codes[:, at:end].bitcast(FP8X4)
            return rest_codes[:, at - FIRST : end - FIRST].bitcast(FP8X4)

        def quantize(b, at, end):
            grouped, scales = (mix, mix_scales) if b == 0 else (w1, w1_scales)
            nc.vector.quantize_mx(
                out=codes_of(b, at, end),
                scales=scales[:, at:end],
                in_=grouped[:, at:end, :].rearrange("p s t -> p (s t)"),
            )

        def multiply(b, e, acc):
            w_scales = mix_scales if b == 0 else w1_scales
            feat = slice(w_at(b, e), w_at(b, e) + P)
            slots = slice(X_AT + e * C, X_AT + (e + 1) * C)
            nc.tensor.matmul_mx(
                out=acc,
                lhsT=codes_of(b, feat.start, feat.stop),
                lhsT_scale=w_scales[:, feat],
                rhs=codes_of(0, slots.start, slots.stop),
                rhs_scale=mix_scales[:, slots],
                start=True,
                stop=True,
            )

        def multiply_half(b, h, y):
            acc = psum.tile([P, HALF], F32, name="acc%d%d" % (b, h))
            for i in range(2):
                multiply(b, 2 * h + i, acc[:, i * C : (i + 1) * C])
            nc.scalar.copy(out=y, in_=acc[:])

        def scatter(h, y):
            nc.vector.tensor_tensor(
                out=windows[0][:].indirect(list_half(h)), in0=y[:], in1=gates[h][:], op=MULT
            )

        for t in range(PACK):
            for h in range(2):
                gather(t, h)
        interleave_w(0, 0)
        interleave_w(0, 1)
        first_codes = keep.tile([P, FIRST], U32, name="first_codes", align_bytes=64)
        quantize(0, 0, FIRST)
        interleave_w(0, 2)
        rest_codes = keep.tile([P, MIX - FIRST], U32, name="rest_codes", tag="turn", align_bytes=64)
        quantize(0, FIRST, FIRST + C)
        y00 = keep.tile([P, HALF], F32, name="y00")
        for e in range(2):
            acc = psum.tile([P, HALF], F32, name="acc00%d" % e)
            multiply(0, e, acc[:, 0:C])
            nc.scalar.copy(out=y00[:, e * C : (e + 1) * C], in_=acc[:, 0:C])
        quantize(0, FIRST + C, W23_AT)
        interleave_w(0, 3)
        quantize(0, W23_AT, MIX)
        scatter(0, y00)
        w1 = keep.tile([P, E * P, PACK], BF16, name="w1", tag="grouped", align_bytes=64)
        interleave_pair()
        for e in range(2, E):
            interleave_w(1, e)
        y01 = keep.tile([P, HALF], F32, name="y01", tag="late", align_bytes=64)
        multiply_half(0, 1, y01[:])
        quantize(1, 0, E * P)
        y1 = keep.tile([P, SLOTS], F32, name="y1")
        for h in range(2):
            multiply_half(1, h, y1[:, h * HALF : (h + 1) * HALF])
        scatter(1, y01)
        nc.sync.dma_start(out[0:P, :], windows[0][:])
        nc.vector.tensor_tensor(out=windows[1][:].indirect(offsets[:]), in0=y1[:], in1=gate1[:], op=MULT)
        nc.sync.dma_start(out[P : 2 * P, :], windows[1][:])
